import numpy as np
import ml_dtypes


def mxq(x, axis, fmt="e4m3"):
    dtype, down = {"e4m3": (ml_dtypes.float8_e4m3fn, 7), "e5m2": (ml_dtypes.float8_e5m2, 14)}[fmt]
    v = np.moveaxis(np.asarray(x, np.float32).astype(ml_dtypes.bfloat16).astype(np.float64), axis, -1)
    blocks = v.reshape(v.shape[:-1] + (-1, 32))
    amax = np.abs(blocks).max(-1, keepdims=True)
    byte = np.maximum(np.where(amax > 0, np.frexp(amax)[1] - 1 + 127, 0) - down, 1)
    scale = np.exp2(byte - 127.0)
    codes = (blocks / scale).astype(np.float32).astype(dtype).astype(np.float64)
    return np.moveaxis((codes * scale).reshape(v.shape), -1, axis)


WIDE = False


def mx_kscale(k):
    if not WIDE:
        return np.ones(k)
    levels = np.array([10, -10, 5, -5, 0])
    if k % 512:
        return np.exp2(np.random.permutation(np.resize(levels, k // 32))).repeat(32)
    a = np.empty((k // 512, 16))
    for p in range(k // 512):
        a[p, :8] = np.random.permutation(np.resize(levels, 8))
        for g in range(8):
            far = levels[np.abs(levels - a[p, g]) >= 10]
            a[p, g + 8] = far[np.random.randint(len(far))]
    return np.exp2(a.ravel()).repeat(32)


def f64(x):
    return np.asarray(x).astype(np.float64)


def striped(idx):
    return np.tile(idx.reshape(-1, 16).T, (8, 1)).astype(np.uint16)


def unstriped(offs):
    return offs[:16].T.reshape(-1).astype(np.int64)


E2M1 = np.array([0.0, 0.5, 1.0, 1.5, 2.0, 3.0, 4.0, 6.0, -0.0, -0.5, -1.0, -1.5, -2.0, -3.0, -4.0, -6.0])


def pack_weight(w, fmt):
    k, n = w.shape
    w = f64(np.asarray(w, np.float32).astype(ml_dtypes.bfloat16)).reshape(k // 32, 32, n)
    amax = np.abs(w).max(1)
    if fmt == "e4m3":
        byte = np.frexp(amax)[1] - 1 + 127 - 7
    else:
        mant, ex = np.frexp(amax / 6.0)
        byte = np.where(mant > 0.5, ex, ex - 1) + 127
    byte = np.clip(np.where(amax > 0, byte, 1), 1, 254)
    scaled = (w * np.exp2(127.0 - byte)[:, None, :]).reshape(k, n).astype(np.float32)
    by_word = np.ascontiguousarray(scaled.reshape(k // 512, 128, 4, n).transpose(0, 1, 3, 2))
    if fmt == "e4m3":
        words = by_word.astype(ml_dtypes.float8_e4m3fn).view(np.uint8)
    else:
        c = by_word.astype(ml_dtypes.float4_e2m1fn).view(np.uint8) & 0xF
        words = (c[..., 0::2] | (c[..., 1::2] << 4)).reshape(k // 512, 128, 2 * n)
    return np.ascontiguousarray(words), np.ascontiguousarray(byte.astype(np.uint8).reshape(k // 512, 16, n))


def unpack_weight(words, scales, fmt):
    g, _, n = scales.shape
    words = np.ascontiguousarray(words).reshape(g, 128, n, -1)
    if fmt == "e4m3":
        vals = words.view(ml_dtypes.float8_e4m3fn).astype(np.float64)
    else:
        nib = np.empty((g, 128, n, 4), np.uint8)
        nib[..., 0::2] = words & 0xF
        nib[..., 1::2] = words >> 4
        vals = E2M1[nib]
    vals = vals * np.repeat(np.exp2(scales.astype(np.float64) - 127.0), 8, axis=1)[..., None]
    return vals.transpose(0, 1, 3, 2).reshape(g * 512, n)


def gelu(v):
    return 0.5 * v * (1.0 + np.tanh(np.sqrt(2.0 / np.pi) * (v + 0.044715 * v**3)))


def bf(x):
    return np.asarray(x, np.float32).astype(ml_dtypes.bfloat16)


def planes(Y):
    n, m = Y.shape
    b = f64(bf(Y)).reshape(n // 32, 32, m)
    amax = np.abs(b).max(1)
    byte = np.clip(np.where(amax > 0, np.frexp(amax)[1] - 1 + 127 - 7, 1), 1, 254)
    codes = (b * np.exp2(127.0 - byte)[:, None, :]).reshape(n, m).astype(np.float32).astype(ml_dtypes.float8_e4m3fn).view(np.uint8)
    words = codes.reshape(n // 512, 128, 4, m).transpose(0, 1, 3, 2)
    return np.ascontiguousarray(words), np.ascontiguousarray(byte.astype(np.uint8).reshape(n // 512, 16, m))


K, T, S, H, N, P = 1024, 2048, 1024, 1536, 512, 512


def setup_inputs():
    n = np.random.standard_normal
    s = mx_kscale(K)[:, None]
    u = mx_kscale(H)[:, None]
    tab_words, tab_scales = pack_weight(n((K, T)) * s, "e4m3")
    w1 = n((K, H)) / s * u.T / np.sqrt(K)
    wa_words, wa_scales = pack_weight(n((H, N)) / u / np.sqrt(H), "e2m1")
    fresh = np.random.uniform(0.5, 1.5, (N, S))
    gain = 5.0 * np.exp(0.8 * n(N))
    return {
        "tab_words": tab_words,
        "tab_scales": tab_scales,
        "offs": striped(np.random.permutation(T)[:S]),
        "pos1": striped(np.random.permutation(S)[:P]),
        "pos2": striped(np.random.permutation(S)[:P]),
        "w1": w1.astype(np.float32),
        "wa_words": wa_words,
        "wa_scales": wa_scales,
        "fresh": fresh.astype(np.float32),
        "gain": gain.astype(np.float32),
    }


def reference(tab_words, tab_scales, offs, pos1, pos2, w1, wa_words, wa_scales, fresh, gain):
    v = unpack_weight(tab_words, tab_scales, "e4m3")[:, unstriped(offs)]
    w1q = mxq(f64(w1), 0, "e4m3")
    wa = unpack_weight(wa_words, wa_scales, "e2m1")
    h = np.maximum(w1q.T @ v, 0.0)
    hq = mxq(h, 0, "e4m3")
    e = (wa.T @ hq) * f64(fresh)
    top = e.max(axis=1)
    a = np.exp(e[:, unstriped(pos1)] - top[:, None])
    c = e[:, unstriped(pos2)]
    y = (f64(gain)[:, None] * a - c) * c
    words, scales = planes(y)
    return y, words, scales

@@ -1,0 +1,268 @@
+from contextlib import ExitStack
+
+import concourse.mybir as mybir
+
+K, T, S, H, N, M = 1024, 2048, 1024, 1536, 512, 512
+FLOPS = 2 * K * H * S + 2 * H * N * S
+
+F32 = mybir.dt.float32
+BF16 = mybir.dt.bfloat16
+I32 = mybir.dt.int32
+U32 = mybir.dt.uint32
+U16 = mybir.dt.uint16
+U8 = mybir.dt.uint8
+FP8X4 = mybir.dt.float8_e4m3fn_x4
+FP4X4 = mybir.dt.float4_e2m1fn_x4
+ACT = mybir.ActivationFunctionType
+ALU = mybir.AluOpType
+AXIS = mybir.AxisListType
+
+P = 128
+PACK = 4
+PASS = P * PACK
+KP = K // PASS
+HP = H // PASS
+CHUNK = 128
+CHUNKS = S // CHUNK
+HALF = S // 2
+BANKS = 8
+
+
+def tile_list_tile_expiry_board_kernel(
+    tc, tab_words, tab_scales, offs, pos1, pos2, w1, wa_words, wa_scales, fresh, gain, out_0, out_1, out_2
+):
+    nc = tc.nc
+    with ExitStack() as ctx:
+        keep = ctx.enter_context(tc.tile_pool(name="keep", bufs=1))
+        ring = ctx.enter_context(tc.tile_pool(name="ring", bufs=3))
+        psum = ctx.enter_context(tc.psum_pool(name="psum", bufs=1))
+
+        def held(name, shape, dtype, tag=""):
+            return keep.tile(shape, dtype, name=name, tag=tag or name, align_bytes=64)
+
+        def bank(i):
+            return psum.tile([P, PASS], F32, name="bank%d" % i)
+
+        offs_sb = keep.tile([P, S // 16], U16, name="offs_sb")
+        pos1_sb = keep.tile([P, M // 16], U16, name="pos1_sb")
+        pos2_sb = keep.tile([P, M // 16], U16, name="pos2_sb")
+        tab_w = [held("tab_w%d" % a, [P, T], U32) for a in range(KP)]
+        tab_s = held("tab_s", [P, T], U8)
+        w_raw = {(a, b): held("w_raw%d%d" % (a, b), [P, PACK, PASS], F32) for a in range(KP) for b in range(HP)}
+        wa_raw_w = held("wa_raw_w", [P, HP, N], U16)
+        wa_raw_s = held("wa_raw_s", [P, HP, N], U8)
+        fresh_sb = [held("fresh%d" % u, [P, PACK, HALF], F32) for u in range(2)]
+        gain_sb = held("gain_sb", [P, PACK], F32)
+
+        nc.vector.memset(tab_s[:].bitcast(I32), 0)
+        nc.vector.memset(wa_raw_s[:].bitcast(I32), 0)
+
+        def load_w1(a, b):
+            rows = w1[a * PASS : (a + 1) * PASS, b * PASS : (b + 1) * PASS]
+            nc.sync.dma_start(out=w_raw[a, b][:], in_=rows.rearrange("(p j) c -> p j c", j=PACK))
+
+        def load_tab(a):
+            nc.sync.dma_start(out=tab_w[a][:].bitcast(I32), in_=tab_words[a].rearrange("p t i -> p (t i)").bitcast(I32))
+
+        nc.sync.dma_start(offs_sb[:], offs)
+        nc.sync.dma_start(out=gain_sb[:], in_=gain.rearrange("(p t) -> p t", t=PACK))
+        for q in range(4):
+            nc.sync.dma_start(
+                out=tab_s[32 * q : 32 * q + 4 * KP, :].bitcast(I32),
+                in_=tab_scales[:, 4 * q : 4 * q + 4, :].bitcast(I32),
+            )
+        load_tab(0)
+        load_w1(0, 0)
+        load_tab(1)
+        load_w1(1, 0)
+        nc.sync.dma_start(pos1_sb[:], pos1)
+        nc.sync.dma_start(pos2_sb[:], pos2)
+        load_w1(0, 1)
+        load_w1(1, 1)
+        nc.sync.dma_start(out=wa_raw_w[:].bitcast(I32), in_=wa_words.rearrange("a p n -> p a n").bitcast(I32))
+        for q in range(4):
+            nc.sync.dma_start(
+                out=wa_raw_s[32 * q : 32 * q + 4, :, :].bitcast(I32),
+                in_=wa_scales[:, 4 * q : 4 * q + 4, :].rearrange("a r n -> r a n").bitcast(I32),
+            )
+        load_w1(0, 2)
+        load_w1(1, 2)
+        fresh_rows = fresh.rearrange("(p t) j -> p t j", t=PACK)
+        for u in range(2):
+            nc.sync.dma_start(out=fresh_sb[u][:], in_=fresh_rows[:, :, u * HALF : (u + 1) * HALF])
+
+        v_w = {}
+        v_s = held("v_s", [P, S], U8)
+
+        def gather_words(a, width, tag=""):
+            v_w[a] = held("v_w%d" % a, [P, S], U32, tag=tag)
+            for j0 in range(0, S, width):
+                picks = offs_sb[:, j0 // 16 : (j0 + width) // 16]
+                nc.vector.tensor_copy(out=v_w[a][:, j0 : j0 + width], in_=tab_w[a][:].indirect(picks))
+
+        w_w = {ab: held("w_w%d%d" % ab, [P, PASS], U32) for ab in w_raw}
+        w_s = {ab: held("w_s%d%d" % ab, [P, PASS], U8) for ab in w_raw}
+
+        def quantize_w1(a, b, scalar_share):
+            if (a, b) == (0, 0):
+                rounded = held("w_first", [P, PASS * PACK], BF16)
+            else:
+                rounded = ring.tile([P, PASS * PACK], BF16, name="w_rounded", align_bytes=64, bufs=2)
+            dst = rounded[:].rearrange("p (t m j) -> p m j t", t=PACK, j=PACK)
+            src = w_raw[a, b][:].rearrange("p j (m t) -> p m j t", t=PACK)
+            if scalar_share > 0:
+                nc.scalar.copy(out=dst[:, :scalar_share], in_=src[:, :scalar_share])
+            if scalar_share < P:
+                nc.vector.tensor_copy(out=dst[:, scalar_share:], in_=src[:, scalar_share:])
+            nc.vector.quantize_mx(out=w_w[a, b][:].bitcast(FP8X4), scales=w_s[a, b][:], in_=rounded[:])
+
+        wa_w = held("wa_w", [P, HP, N], U16, tag="w_raw11")
+        wa_s = held("wa_s", [P, HP, N], U8, tag="w_raw01")
+
+        def deal_wa():
+            for b in range(HP):
+                for dealt, raw in ((wa_s, wa_raw_s), (wa_w, wa_raw_w)):
+                    nc.vector.tensor_copy(
+                        out=dealt[:, b, :].rearrange("p (t m) -> p m t", t=PACK),
+                        in_=raw[:, b, :].rearrange("p (m t) -> p m t", t=PACK),
+                    )
+
+        h_w = {}
+        h_s = {(b, u): held("h_s%d%d" % (b, u), [P, HALF], U8) for b in range(HP) for u in range(2)}
+
+        def first_pass(acc, a, b, c):
+            cols = slice(c * CHUNK, (c + 1) * CHUNK)
+            for t in range(PACK):
+                rows = slice(t * P, (t + 1) * P)
+                nc.tensor.matmul_mx(
+                    out=acc[:, t * CHUNK : (t + 1) * CHUNK],
+                    lhsT=w_w[a, b][:, rows].bitcast(FP8X4),
+                    lhsT_scale=w_s[a, b][:, rows],
+                    rhs=v_w[a][:, cols].bitcast(FP8X4),
+                    rhs_scale=v_s[4 * a : P, cols],
+                    start=(a == 0 and t == 0),
+                    stop=(a == KP - 1 and t == PACK - 1),
+                )
+
+        def relu_out(acc, rounded, c, on_scalar):
+            dst = rounded[:, (c % 4) * PASS : (c % 4 + 1) * PASS].rearrange("p (n t) -> p n t", t=PACK)
+            src = acc[:].rearrange("p (t n) -> p n t", t=PACK)
+            if on_scalar:
+                nc.scalar.activation(out=dst, in_=src, func=ACT.Relu)
+            else:
+                nc.vector.tensor_scalar_max(out=dst, in0=src, scalar1=0.0)
+
+        def quantize_h(rounded, b, u):
+            if u == 0:
+                h_w[b] = held("h_w%d" % b, [P, 2, HALF], U32, tag="w_raw%d%d" % ((b, HP - 1) if b < KP else (0, 0)))
+            nc.vector.quantize_mx(out=h_w[b][:, u, :].bitcast(FP8X4), scales=h_s[b, u][:], in_=rounded[:])
+
+        def second_pass(acc, b, t, u):
+            rows = slice(t * P, (t + 1) * P)
+            nc.tensor.matmul_mx(
+                out=acc[:],
+                lhsT=wa_w[:, b, rows].bitcast(FP4X4),
+                lhsT_scale=wa_s[:, b, rows],
+                rhs=h_w[b][:, u, :].bitcast(FP8X4),
+                rhs_scale=h_s[b, u][:],
+                start=(b == 0),
+                stop=(b == HP - 1),
+            )
+
+        nc.vector.tensor_copy(out=v_s[:], in_=tab_s[:].indirect(offs_sb[:]))
+        gather_words(0, S)
+        quantize_w1(0, 0, 48)
+        gather_words(1, S, tag="w_first")
+        quantize_w1(1, 0, 48)
+
+        def round_half(accs, b, u, vector_chunks):
+            rounded = ring.tile([P, HALF * PACK], BF16, name="h_rounded", align_bytes=64, bufs=5)
+            for c in range(4 * u, 4 * u + 4):
+                first_pass(accs[c], KP - 1, b, c)
+                relu_out(accs[c], rounded, c, c not in vector_chunks)
+            return rounded
+
+        last = HP - 1
+        for b in range(last):
+            accs = {c: bank(c) for c in range(CHUNKS)}
+            for c in range(CHUNKS):
+                first_pass(accs[c], 0, b, c)
+            halves = [round_half(accs, b, u, ()) for u in range(2)]
+            quantize_w1(0, b + 1, 0)
+            quantize_w1(1, b + 1, 0)
+            if b == 0:
+                deal_wa()
+            for u in range(2):
+                quantize_h(halves[u], b, u)
+
+        e_sb = [held("e%d" % t, [P, S], F32) for t in range(PACK)]
+        half_top = held("half_top", [P, PACK, 2], F32)
+        neg_top = held("neg_top", [P, PACK], F32)
+
+        def scores_out(acc, t, u):
+            cols = slice(u * HALF, (u + 1) * HALF)
+            nc.vector.tensor_tensor(out=e_sb[t][:, cols], in0=acc[:], in1=fresh_sb[u][:, t, :], op=ALU.mult)
+
+        def half_max(t, u):
+            cols = slice(u * HALF, (u + 1) * HALF)
+            nc.vector.tensor_reduce(out=half_top[:, t, u : u + 1], in_=e_sb[t][:, cols], axis=AXIS.X, op=ALU.max)
+
+        accs = {c: bank(c) for c in range(4)}
+        for c in range(4):
+            first_pass(accs[c], 0, last, c)
+        e_acc = {t: bank(4 + t) for t in range(PACK)}
+        for t in range(PACK):
+            second_pass(e_acc[t], 0, t, 0)
+        rounded = round_half(accs, last, 0, (3,))
+        quantize_h(rounded, last, 0)
+        for t in range(PACK):
+            second_pass(e_acc[t], 1, t, 0)
+        for t in range(PACK):
+            second_pass(e_acc[t], last, t, 0)
+        rounded = ring.tile([P, HALF * PACK], BF16, name="h_rounded", align_bytes=64, bufs=5)
+        for c in range(4, CHUNKS):
+            acc = bank(c - 4)
+            first_pass(acc, 0, last, c)
+            first_pass(acc, 1, last, c)
+            relu_out(acc, rounded, c, True)
+        quantize_h(rounded, last, 1)
+        for t in range(PACK):
+            scores_out(e_acc[t], t, 0)
+
+        y_sb = held("y_sb", [P, PACK, M], F32)
+        y_rows = out_0.rearrange("(p t) m -> p t m", t=PACK)
+        for t in range(PACK):
+            acc = bank(4 + t)
+            for b in range(HP):
+                second_pass(acc, b, t, 1)
+            half_max(t, 0)
+            scores_out(acc, t, 1)
+            half_max(t, 1)
+            nc.vector.tensor_reduce(out=neg_top[:, t : t + 1], in_=half_top[:, t, :], axis=AXIS.X, op=ALU.max, negate=True)
+            a_sb = ring.tile([P, M], F32, name="a_sb")
+            nc.scalar.activation(
+                out=a_sb[:], in_=e_sb[t][:].indirect(pos1_sb[:]), func=ACT.Exp, bias=neg_top[:, t : t + 1]
+            )
+            c_sb = ring.tile([P, M], F32, name="c_sb")
+            nc.vector.tensor_copy(out=c_sb[:], in_=e_sb[t][:].indirect(pos2_sb[:]))
+            d_sb = ring.tile([P, M], F32, name="d_sb")
+            nc.vector.scalar_tensor_tensor(
+                out=d_sb[:], in0=a_sb[:], scalar=gain_sb[:, t : t + 1], in1=c_sb[:], op0=ALU.mult, op1=ALU.subtract
+            )
+            nc.vector.tensor_tensor(out=y_sb[:, t, :], in0=d_sb[:], in1=c_sb[:], op=ALU.mult)
+            nc.sync.dma_start(out=y_rows[:, t, :], in_=y_sb[:, t, :])
+
+        y_rounded = held("y_rounded", [P, M * PACK], BF16)
+        y_w = held("y_w", [P, M], U32)
+        y_s = held("y_s", [P, M], U8)
+        split = 160
+        for lo, hi, copy in ((0, split, nc.scalar.copy), (split, M, nc.vector.tensor_copy)):
+            copy(
+                out=y_rounded[:, lo * PACK : hi * PACK].rearrange("p (c i t) -> p c t i", i=4, t=PACK),
+                in_=y_sb[:, :, lo:hi].rearrange("p t (c i) -> p c t i", i=4),
+            )
+        nc.vector.quantize_mx(out=y_w[:].bitcast(FP8X4), scales=y_s[:], in_=y_rounded[:])
+        nc.sync.dma_start(out=out_1[0].rearrange("p m t -> p (m t)").bitcast(I32), in_=y_w[:].bitcast(I32))
+        for q in range(4):
+            queue = nc.scalar if q % 2 == 0 else nc.sync
+            queue.dma_start(out=out_2[0, 4 * q : 4 * q + 4, :].bitcast(I32), in_=y_s[32 * q : 32 * q + 4, :].bitcast(I32))

@@ -73,20 +73,20 @@ def tile_list_tile_expiry_board_kernel(
             )
         load_tab(0)
         load_w1(0, 0)
-        load_tab(1)
         load_w1(1, 0)
+        load_tab(1)
         nc.sync.dma_start(pos1_sb[:], pos1)
         nc.sync.dma_start(pos2_sb[:], pos2)
         load_w1(0, 1)
         load_w1(1, 1)
+        load_w1(0, 2)
+        load_w1(1, 2)
         nc.sync.dma_start(out=wa_raw_w[:].bitcast(I32), in_=wa_words.rearrange("a p n -> p a n").bitcast(I32))
         for q in range(4):
             nc.sync.dma_start(
                 out=wa_raw_s[32 * q : 32 * q + 4, :, :].bitcast(I32),
                 in_=wa_scales[:, 4 * q : 4 * q + 4, :].rearrange("a r n -> r a n").bitcast(I32),
             )
-        load_w1(0, 2)
-        load_w1(1, 2)
         fresh_rows = fresh.rearrange("(p t) j -> p t j", t=PACK)
         for u in range(2):
             nc.sync.dma_start(out=fresh_sb[u][:], in_=fresh_rows[:, :, u * HALF : (u + 1) * HALF])
@@ -104,8 +104,10 @@ def tile_list_tile_expiry_board_kernel(
         w_s = {ab: held("w_s%d%d" % ab, [P, PASS], U8) for ab in w_raw}
 
         def quantize_w1(a, b, scalar_share):
-            if (a, b) == (0, 0):
-                rounded = held("w_first", [P, PASS * PACK], BF16)
+            if b == 0:
+                rounded = held("w_rounded%d%d" % (a, b), [P, PASS * PACK], BF16, tag="w_first")
+            elif (a, b) == (1, 2):
+                rounded = held("w_rounded12", [P, PASS * PACK], BF16)
             else:
                 rounded = ring.tile([P, PASS * PACK], BF16, name="w_rounded", align_bytes=64, bufs=2)
             dst = rounded[:].rearrange("p (t m j) -> p m j t", t=PACK, j=PACK)
@@ -116,18 +118,17 @@ def tile_list_tile_expiry_board_kernel(
                 nc.vector.tensor_copy(out=dst[:, scalar_share:], in_=src[:, scalar_share:])
             nc.vector.quantize_mx(out=w_w[a, b][:].bitcast(FP8X4), scales=w_s[a, b][:], in_=rounded[:])
 
-        wa_w = held("wa_w", [P, HP, N], U16, tag="w_raw11")
-        wa_s = held("wa_s", [P, HP, N], U8, tag="w_raw01")
+        wa_w = held("wa_w", [P, HP, N], U16, tag="w_raw12")
+        wa_s = held("wa_s", [P, HP, N], U8, tag="wa_raw_w")
 
         def deal_wa():
-            for b in range(HP):
-                for dealt, raw in ((wa_s, wa_raw_s), (wa_w, wa_raw_w)):
-                    nc.vector.tensor_copy(
-                        out=dealt[:, b, :].rearrange("p (t m) -> p m t", t=PACK),
-                        in_=raw[:, b, :].rearrange("p (m t) -> p m t", t=PACK),
-                    )
+            for dealt, raw in ((wa_w, wa_raw_w), (wa_s, wa_raw_s)):
+                nc.vector.tensor_copy(
+                    out=dealt[:].rearrange("p b (t h m) -> p h b m t", t=PACK, h=2),
+                    in_=raw[:].rearrange("p b (h m t) -> p h b m t", t=PACK, h=2),
+                )
 
-        h_w = {}
+        h_w = [held("h_w%d" % b, [P, 2, HALF], U32, tag=tag) for b, tag in enumerate(("w_raw02", "w_rounded12", ""))]
         h_s = {(b, u): held("h_s%d%d" % (b, u), [P, HALF], U8) for b in range(HP) for u in range(2)}
 
         def first_pass(acc, a, b, c):
@@ -144,17 +145,12 @@ def tile_list_tile_expiry_board_kernel(
                     stop=(a == KP - 1 and t == PACK - 1),
                 )
 
-        def relu_out(acc, rounded, c, on_scalar):
+        def relu_out(acc, rounded, c):
             dst = rounded[:, (c % 4) * PASS : (c % 4 + 1) * PASS].rearrange("p (n t) -> p n t", t=PACK)
             src = acc[:].rearrange("p (t n) -> p n t", t=PACK)
-            if on_scalar:
-                nc.scalar.activation(out=dst, in_=src, func=ACT.Relu)
-            else:
-                nc.vector.tensor_scalar_max(out=dst, in0=src, scalar1=0.0)
+            nc.scalar.activation(out=dst, in_=src, func=ACT.Relu)
 
         def quantize_h(rounded, b, u):
-            if u == 0:
-                h_w[b] = held("h_w%d" % b, [P, 2, HALF], U32, tag="w_raw%d%d" % ((b, HP - 1) if b < KP else (0, 0)))
             nc.vector.quantize_mx(out=h_w[b][:, u, :].bitcast(FP8X4), scales=h_s[b, u][:], in_=rounded[:])
 
         def second_pass(acc, b, t, u):
@@ -172,73 +168,42 @@ def tile_list_tile_expiry_board_kernel(
         nc.vector.tensor_copy(out=v_s[:], in_=tab_s[:].indirect(offs_sb[:]))
         gather_words(0, S)
         quantize_w1(0, 0, 48)
-        gather_words(1, S, tag="w_first")
         quantize_w1(1, 0, 48)
+        gather_words(1, 256, tag="w_first")
 
-        def round_half(accs, b, u, vector_chunks):
-            rounded = ring.tile([P, HALF * PACK], BF16, name="h_rounded", align_bytes=64, bufs=5)
-            for c in range(4 * u, 4 * u + 4):
-                first_pass(accs[c], KP - 1, b, c)
-                relu_out(accs[c], rounded, c, c not in vector_chunks)
-            return rounded
-
-        last = HP - 1
-        for b in range(last):
+        for b in range(HP):
             accs = {c: bank(c) for c in range(CHUNKS)}
             for c in range(CHUNKS):
                 first_pass(accs[c], 0, b, c)
-            halves = [round_half(accs, b, u, ()) for u in range(2)]
-            quantize_w1(0, b + 1, 0)
-            quantize_w1(1, b + 1, 0)
-            if b == 0:
+            halves = [held("h_rounded%d%d" % (b, u), [P, HALF * PACK], BF16) for u in range(2)]
+            for c in range(CHUNKS):
+                first_pass(accs[c], 1, b, c)
+                relu_out(accs[c], halves[c // 4], c)
+            if b + 1 < HP:
+                quantize_w1(0, b + 1, 0)
+                quantize_w1(1, b + 1, 0)
+            if b == 1:
                 deal_wa()
             for u in range(2):
                 quantize_h(halves[u], b, u)
 
         e_sb = [held("e%d" % t, [P, S], F32) for t in range(PACK)]
-        half_top = held("half_top", [P, PACK, 2], F32)
         neg_top = held("neg_top", [P, PACK], F32)
-
-        def scores_out(acc, t, u):
-            cols = slice(u * HALF, (u + 1) * HALF)
-            nc.vector.tensor_tensor(out=e_sb[t][:, cols], in0=acc[:], in1=fresh_sb[u][:, t, :], op=ALU.mult)
-
-        def half_max(t, u):
-            cols = slice(u * HALF, (u + 1) * HALF)
-            nc.vector.tensor_reduce(out=half_top[:, t, u : u + 1], in_=e_sb[t][:, cols], axis=AXIS.X, op=ALU.max)
-
-        accs = {c: bank(c) for c in range(4)}
-        for c in range(4):
-            first_pass(accs[c], 0, last, c)
-        e_acc = {t: bank(4 + t) for t in range(PACK)}
-        for t in range(PACK):
-            second_pass(e_acc[t], 0, t, 0)
-        rounded = round_half(accs, last, 0, (3,))
-        quantize_h(rounded, last, 0)
-        for t in range(PACK):
-            second_pass(e_acc[t], 1, t, 0)
-        for t in range(PACK):
-            second_pass(e_acc[t], last, t, 0)
-        rounded = ring.tile([P, HALF * PACK], BF16, name="h_rounded", align_bytes=64, bufs=5)
-        for c in range(4, CHUNKS):
-            acc = bank(c - 4)
-            first_pass(acc, 0, last, c)
-            first_pass(acc, 1, last, c)
-            relu_out(acc, rounded, c, True)
-        quantize_h(rounded, last, 1)
-        for t in range(PACK):
-            scores_out(e_acc[t], t, 0)
-
         y_sb = held("y_sb", [P, PACK, M], F32)
         y_rows = out_0.rearrange("(p t) m -> p t m", t=PACK)
         for t in range(PACK):
-            acc = bank(4 + t)
-            for b in range(HP):
-                second_pass(acc, b, t, 1)
-            half_max(t, 0)
-            scores_out(acc, t, 1)
-            half_max(t, 1)
-            nc.vector.tensor_reduce(out=neg_top[:, t : t + 1], in_=half_top[:, t, :], axis=AXIS.X, op=ALU.max, negate=True)
+            for u in range(2):
+                acc = bank(2 * t + u)
+                for b in range(HP):
+                    second_pass(acc, b, t, u)
+                scores = e_sb[t][:, u * HALF : (u + 1) * HALF]
+                if u == 0 and t > 0:
+                    sums = ring.tile([P, HALF], F32, name="sums")
+                    nc.scalar.copy(out=sums[:], in_=acc[:])
+                    nc.gpsimd.tensor_tensor(out=scores, in0=sums[:], in1=fresh_sb[u][:, t, :], op=ALU.mult)
+                else:
+                    nc.vector.tensor_tensor(out=scores, in0=acc[:], in1=fresh_sb[u][:, t, :], op=ALU.mult)
+            nc.vector.tensor_reduce(out=neg_top[:, t : t + 1], in_=e_sb[t][:], axis=AXIS.X, op=ALU.max, negate=True)
             a_sb = ring.tile([P, M], F32, name="a_sb")
             nc.scalar.activation(
                 out=a_sb[:], in_=e_sb[t][:].indirect(pos1_sb[:]), func=ACT.Exp, bias=neg_top[:, t : t + 1]
@@ -246,10 +211,16 @@ def tile_list_tile_expiry_board_kernel(
             c_sb = ring.tile([P, M], F32, name="c_sb")
             nc.vector.tensor_copy(out=c_sb[:], in_=e_sb[t][:].indirect(pos2_sb[:]))
             d_sb = ring.tile([P, M], F32, name="d_sb")
-            nc.vector.scalar_tensor_tensor(
-                out=d_sb[:], in0=a_sb[:], scalar=gain_sb[:, t : t + 1], in1=c_sb[:], op0=ALU.mult, op1=ALU.subtract
-            )
-            nc.vector.tensor_tensor(out=y_sb[:, t, :], in0=d_sb[:], in1=c_sb[:], op=ALU.mult)
+            if t + 1 < PACK:
+                ga_sb = ring.tile([P, M], F32, name="ga_sb")
+                nc.scalar.activation(out=ga_sb[:], in_=a_sb[:], func=ACT.Copy, scale=gain_sb[:, t : t + 1])
+                nc.gpsimd.tensor_tensor(out=d_sb[:], in0=ga_sb[:], in1=c_sb[:], op=ALU.subtract)
+                nc.gpsimd.tensor_tensor(out=y_sb[:, t, :], in0=d_sb[:], in1=c_sb[:], op=ALU.mult)
+            else:
+                nc.vector.scalar_tensor_tensor(
+                    out=d_sb[:], in0=a_sb[:], scalar=gain_sb[:, t : t + 1], in1=c_sb[:], op0=ALU.mult, op1=ALU.subtract
+                )
+                nc.vector.tensor_tensor(out=y_sb[:, t, :], in0=d_sb[:], in1=c_sb[:], op=ALU.mult)
             nc.sync.dma_start(out=y_rows[:, t, :], in_=y_sb[:, t, :])
 
         y_rounded = held("y_rounded", [P, M * PACK], BF16)

@@ -145,10 +145,13 @@ def tile_list_tile_expiry_board_kernel(
                     stop=(a == KP - 1 and t == PACK - 1),
                 )
 
-        def relu_out(acc, rounded, c):
+        def relu_out(acc, rounded, c, on_scalar):
             dst = rounded[:, (c % 4) * PASS : (c % 4 + 1) * PASS].rearrange("p (n t) -> p n t", t=PACK)
             src = acc[:].rearrange("p (t n) -> p n t", t=PACK)
-            nc.scalar.activation(out=dst, in_=src, func=ACT.Relu)
+            if on_scalar:
+                nc.scalar.activation(out=dst, in_=src, func=ACT.Relu)
+            else:
+                nc.vector.tensor_scalar_max(out=dst, in0=src, scalar1=0.0)
 
         def quantize_h(rounded, b, u):
             nc.vector.quantize_mx(out=h_w[b][:, u, :].bitcast(FP8X4), scales=h_s[b, u][:], in_=rounded[:])
@@ -178,7 +181,7 @@ def tile_list_tile_expiry_board_kernel(
             halves = [held("h_rounded%d%d" % (b, u), [P, HALF * PACK], BF16) for u in range(2)]
             for c in range(CHUNKS):
                 first_pass(accs[c], 1, b, c)
-                relu_out(accs[c], halves[c // 4], c)
+                relu_out(accs[c], halves[c // 4], c, (b, c) != (HP - 1, CHUNKS - 1))
             if b + 1 < HP:
                 quantize_w1(0, b + 1, 0)
                 quantize_w1(1, b + 1, 0)
@@ -191,6 +194,7 @@ def tile_list_tile_expiry_board_kernel(
         neg_top = held("neg_top", [P, PACK], F32)
         y_sb = held("y_sb", [P, PACK, M], F32)
         y_rows = out_0.rearrange("(p t) m -> p t m", t=PACK)
+        y_halves = [slice(0, M // 2), slice(M // 2, M)]
         for t in range(PACK):
             for u in range(2):
                 acc = bank(2 * t + u)
@@ -211,29 +215,34 @@ def tile_list_tile_expiry_board_kernel(
             c_sb = ring.tile([P, M], F32, name="c_sb")
             nc.vector.tensor_copy(out=c_sb[:], in_=e_sb[t][:].indirect(pos2_sb[:]))
             d_sb = ring.tile([P, M], F32, name="d_sb")
-            if t + 1 < PACK:
+            if t < 2:
                 ga_sb = ring.tile([P, M], F32, name="ga_sb")
                 nc.scalar.activation(out=ga_sb[:], in_=a_sb[:], func=ACT.Copy, scale=gain_sb[:, t : t + 1])
                 nc.gpsimd.tensor_tensor(out=d_sb[:], in0=ga_sb[:], in1=c_sb[:], op=ALU.subtract)
                 nc.gpsimd.tensor_tensor(out=y_sb[:, t, :], in0=d_sb[:], in1=c_sb[:], op=ALU.mult)
             else:
-                nc.vector.scalar_tensor_tensor(
-                    out=d_sb[:], in0=a_sb[:], scalar=gain_sb[:, t : t + 1], in1=c_sb[:], op0=ALU.mult, op1=ALU.subtract
-                )
-                nc.vector.tensor_tensor(out=y_sb[:, t, :], in0=d_sb[:], in1=c_sb[:], op=ALU.mult)
+                parts = y_halves if t + 1 == PACK else [slice(0, M)]
+                for cols in parts:
+                    nc.vector.scalar_tensor_tensor(
+                        out=d_sb[:, cols], in0=a_sb[:, cols], scalar=gain_sb[:, t : t + 1], in1=c_sb[:, cols],
+                        op0=ALU.mult, op1=ALU.subtract,
+                    )
+                for cols in parts:
+                    nc.vector.tensor_tensor(out=y_sb[:, t, cols], in0=d_sb[:, cols], in1=c_sb[:, cols], op=ALU.mult)
             nc.sync.dma_start(out=y_rows[:, t, :], in_=y_sb[:, t, :])
 
-        y_rounded = held("y_rounded", [P, M * PACK], BF16)
         y_w = held("y_w", [P, M], U32)
         y_s = held("y_s", [P, M], U8)
-        split = 160
-        for lo, hi, copy in ((0, split, nc.scalar.copy), (split, M, nc.vector.tensor_copy)):
+        y_rounded = [held("y_rounded%d" % i, [P, M // 2 * PACK], BF16) for i in range(2)]
+        for rounded, cols, copy in zip(y_rounded, y_halves, (nc.scalar.copy, nc.vector.tensor_copy)):
             copy(
-                out=y_rounded[:, lo * PACK : hi * PACK].rearrange("p (c i t) -> p c t i", i=4, t=PACK),
-                in_=y_sb[:, :, lo:hi].rearrange("p t (c i) -> p c t i", i=4),
+                out=rounded[:].rearrange("p (c i t) -> p c t i", i=4, t=PACK),
+                in_=y_sb[:, :, cols].rearrange("p t (c i) -> p c t i", i=4),
             )
-        nc.vector.quantize_mx(out=y_w[:].bitcast(FP8X4), scales=y_s[:], in_=y_rounded[:])
-        nc.sync.dma_start(out=out_1[0].rearrange("p m t -> p (m t)").bitcast(I32), in_=y_w[:].bitcast(I32))
+        words_out = out_1[0].rearrange("p m t -> p (m t)").bitcast(I32)
+        for rounded, cols in reversed(list(zip(y_rounded, y_halves))):
+            nc.vector.quantize_mx(out=y_w[:, cols].bitcast(FP8X4), scales=y_s[:, cols], in_=rounded[:])
+            nc.sync.dma_start(out=words_out[:, cols], in_=y_w[:, cols].bitcast(I32))
         for q in range(4):
             queue = nc.scalar if q % 2 == 0 else nc.sync
             queue.dma_start(out=out_2[0, 4 * q : 4 * q + 4, :].bitcast(I32), in_=y_s[32 * q : 32 * q + 4, :].bitcast(I32))

from contextlib import ExitStack

import concourse.mybir as mybir

K, T, S, H, N, M = 1024, 2048, 1024, 1536, 512, 512
FLOPS = 2 * K * H * S + 2 * H * N * S

F32 = mybir.dt.float32
BF16 = mybir.dt.bfloat16
I32 = mybir.dt.int32
U32 = mybir.dt.uint32
U16 = mybir.dt.uint16
U8 = mybir.dt.uint8
FP8X4 = mybir.dt.float8_e4m3fn_x4
FP4X4 = mybir.dt.float4_e2m1fn_x4
ACT = mybir.ActivationFunctionType
ALU = mybir.AluOpType
AXIS = mybir.AxisListType

P = 128
PACK = 4
PASS = P * PACK
KP = K // PASS
HP = H // PASS
CHUNK = 128
CHUNKS = S // CHUNK
HALF = S // 2
BANKS = 8


def tile_list_tile_expiry_board_kernel(
    tc, tab_words, tab_scales, offs, pos1, pos2, w1, wa_words, wa_scales, fresh, gain, out_0, out_1, out_2
):
    nc = tc.nc
    with ExitStack() as ctx:
        keep = ctx.enter_context(tc.tile_pool(name="keep", bufs=1))
        ring = ctx.enter_context(tc.tile_pool(name="ring", bufs=3))
        psum = ctx.enter_context(tc.psum_pool(name="psum", bufs=1))

        def held(name, shape, dtype, tag=""):
            return keep.tile(shape, dtype, name=name, tag=tag or name, align_bytes=64)

        def bank(i):
            return psum.tile([P, PASS], F32, name="bank%d" % i)

        offs_sb = keep.tile([P, S // 16], U16, name="offs_sb")
        pos1_sb = keep.tile([P, M // 16], U16, name="pos1_sb")
        pos2_sb = keep.tile([P, M // 16], U16, name="pos2_sb")
        tab_w = [held("tab_w%d" % a, [P, T], U32) for a in range(KP)]
        tab_s = held("tab_s", [P, T], U8)
        w_raw = {(a, b): held("w_raw%d%d" % (a, b), [P, PACK, PASS], F32) for a in range(KP) for b in range(HP)}
        wa_raw_w = held("wa_raw_w", [P, HP, N], U16)
        wa_raw_s = held("wa_raw_s", [P, HP, N], U8)
        fresh_sb = [held("fresh%d" % u, [P, PACK, HALF], F32) for u in range(2)]
        gain_sb = held("gain_sb", [P, PACK], F32)

        nc.vector.memset(tab_s[:].bitcast(I32), 0)
        nc.vector.memset(wa_raw_s[:].bitcast(I32), 0)

        def load_w1(a, b):
            rows = w1[a * PASS : (a + 1) * PASS, b * PASS : (b + 1) * PASS]
            nc.sync.dma_start(out=w_raw[a, b][:], in_=rows.rearrange("(p j) c -> p j c", j=PACK))

        def load_tab(a):
            nc.sync.dma_start(out=tab_w[a][:].bitcast(I32), in_=tab_words[a].rearrange("p t i -> p (t i)").bitcast(I32))

        nc.sync.dma_start(offs_sb[:], offs)
        nc.sync.dma_start(out=gain_sb[:], in_=gain.rearrange("(p t) -> p t", t=PACK))
        for q in range(4):
            nc.sync.dma_start(
                out=tab_s[32 * q : 32 * q + 4 * KP, :].bitcast(I32),
                in_=tab_scales[:, 4 * q : 4 * q + 4, :].bitcast(I32),
            )
        load_tab(0)
        load_w1(0, 0)
        load_w1(1, 0)
        load_tab(1)
        nc.sync.dma_start(pos1_sb[:], pos1)
        nc.sync.dma_start(pos2_sb[:], pos2)
        load_w1(0, 1)
        load_w1(1, 1)
        load_w1(0, 2)
        load_w1(1, 2)
        nc.sync.dma_start(out=wa_raw_w[:].bitcast(I32), in_=wa_words.rearrange("a p n -> p a n").bitcast(I32))
        for q in range(4):
            nc.sync.dma_start(
                out=wa_raw_s[32 * q : 32 * q + 4, :, :].bitcast(I32),
                in_=wa_scales[:, 4 * q : 4 * q + 4, :].rearrange("a r n -> r a n").bitcast(I32),
            )
        fresh_rows = fresh.rearrange("(p t) j -> p t j", t=PACK)
        for u in range(2):
            nc.sync.dma_start(out=fresh_sb[u][:], in_=fresh_rows[:, :, u * HALF : (u + 1) * HALF])

        v_w = {}
        v_s = held("v_s", [P, S], U8)

        def gather_words(a, width, tag=""):
            v_w[a] = held("v_w%d" % a, [P, S], U32, tag=tag)
            for j0 in range(0, S, width):
                picks = offs_sb[:, j0 // 16 : (j0 + width) // 16]
                nc.vector.tensor_copy(out=v_w[a][:, j0 : j0 + width], in_=tab_w[a][:].indirect(picks))

        w_w = {ab: held("w_w%d%d" % ab, [P, PASS], U32) for ab in w_raw}
        w_s = {ab: held("w_s%d%d" % ab, [P, PASS], U8) for ab in w_raw}

        def quantize_w1(a, b, scalar_share):
            if b == 0:
                rounded = held("w_rounded%d%d" % (a, b), [P, PASS * PACK], BF16, tag="w_first")
            elif (a, b) == (1, 2):
                rounded = held("w_rounded12", [P, PASS * PACK], BF16)
            else:
                rounded = ring.tile([P, PASS * PACK], BF16, name="w_rounded", align_bytes=64, bufs=2)
            dst = rounded[:].rearrange("p (t m j) -> p m j t", t=PACK, j=PACK)
            src = w_raw[a, b][:].rearrange("p j (m t) -> p m j t", t=PACK)
            if scalar_share > 0:
                nc.scalar.copy(out=dst[:, :scalar_share], in_=src[:, :scalar_share])
            if scalar_share < P:
                nc.vector.tensor_copy(out=dst[:, scalar_share:], in_=src[:, scalar_share:])
            nc.vector.quantize_mx(out=w_w[a, b][:].bitcast(FP8X4), scales=w_s[a, b][:], in_=rounded[:])

        wa_w = held("wa_w", [P, HP, N], U16, tag="w_raw12")
        wa_s = held("wa_s", [P, HP, N], U8, tag="wa_raw_w")

        def deal_wa():
            for dealt, raw in ((wa_w, wa_raw_w), (wa_s, wa_raw_s)):
                nc.vector.tensor_copy(
                    out=dealt[:].rearrange("p b (t h m) -> p h b m t", t=PACK, h=2),
                    in_=raw[:].rearrange("p b (h m t) -> p h b m t", t=PACK, h=2),
                )

        h_w = [held("h_w%d" % b, [P, 2, HALF], U32, tag=tag) for b, tag in enumerate(("w_raw02", "w_rounded12", ""))]
        h_s = {(b, u): held("h_s%d%d" % (b, u), [P, HALF], U8) for b in range(HP) for u in range(2)}

        def first_pass(acc, a, b, c):
            cols = slice(c * CHUNK, (c + 1) * CHUNK)
            for t in range(PACK):
                rows = slice(t * P, (t + 1) * P)
                nc.tensor.matmul_mx(
                    out=acc[:, t * CHUNK : (t + 1) * CHUNK],
                    lhsT=w_w[a, b][:, rows].bitcast(FP8X4),
                    lhsT_scale=w_s[a, b][:, rows],
                    rhs=v_w[a][:, cols].bitcast(FP8X4),
                    rhs_scale=v_s[4 * a : P, cols],
                    start=(a == 0 and t == 0),
                    stop=(a == KP - 1 and t == PACK - 1),
                )

        def relu_out(acc, rounded, c, on_scalar):
            dst = rounded[:, (c % 4) * PASS : (c % 4 + 1) * PASS].rearrange("p (n t) -> p n t", t=PACK)
            src = acc[:].rearrange("p (t n) -> p n t", t=PACK)
            if on_scalar:
                nc.scalar.activation(out=dst, in_=src, func=ACT.Relu)
            else:
                nc.vector.tensor_scalar_max(out=dst, in0=src, scalar1=0.0)

        def quantize_h(rounded, b, u):
            nc.vector.quantize_mx(out=h_w[b][:, u, :].bitcast(FP8X4), scales=h_s[b, u][:], in_=rounded[:])

        def second_pass(acc, b, t, u):
            rows = slice(t * P, (t + 1) * P)
            nc.tensor.matmul_mx(
                out=acc[:],
                lhsT=wa_w[:, b, rows].bitcast(FP4X4),
                lhsT_scale=wa_s[:, b, rows],
                rhs=h_w[b][:, u, :].bitcast(FP8X4),
                rhs_scale=h_s[b, u][:],
                start=(b == 0),
                stop=(b == HP - 1),
            )

        nc.vector.tensor_copy(out=v_s[:], in_=tab_s[:].indirect(offs_sb[:]))
        gather_words(0, S)
        quantize_w1(0, 0, 48)
        quantize_w1(1, 0, 48)
        gather_words(1, 256, tag="w_first")

        for b in range(HP):
            accs = {c: bank(c) for c in range(CHUNKS)}
            for c in range(CHUNKS):
                first_pass(accs[c], 0, b, c)
            halves = [held("h_rounded%d%d" % (b, u), [P, HALF * PACK], BF16) for u in range(2)]
            for c in range(CHUNKS):
                first_pass(accs[c], 1, b, c)
                relu_out(accs[c], halves[c // 4], c, (b, c) != (HP - 1, CHUNKS - 1))
            if b + 1 < HP:
                quantize_w1(0, b + 1, 0)
                quantize_w1(1, b + 1, 0)
            if b == 1:
                deal_wa()
            for u in range(2):
                quantize_h(halves[u], b, u)

        e_sb = [held("e%d" % t, [P, S], F32) for t in range(PACK)]
        neg_top = held("neg_top", [P, PACK], F32)
        y_sb = held("y_sb", [P, PACK, M], F32)
        y_rows = out_0.rearrange("(p t) m -> p t m", t=PACK)
        y_halves = [slice(0, M // 2), slice(M // 2, M)]
        for t in range(PACK):
            for u in range(2):
                acc = bank(2 * t + u)
                for b in range(HP):
                    second_pass(acc, b, t, u)
                scores = e_sb[t][:, u * HALF : (u + 1) * HALF]
                if u == 0 and t > 0:
                    sums = ring.tile([P, HALF], F32, name="sums")
                    nc.scalar.copy(out=sums[:], in_=acc[:])
                    nc.gpsimd.tensor_tensor(out=scores, in0=sums[:], in1=fresh_sb[u][:, t, :], op=ALU.mult)
                else:
                    nc.vector.tensor_tensor(out=scores, in0=acc[:], in1=fresh_sb[u][:, t, :], op=ALU.mult)
            nc.vector.tensor_reduce(out=neg_top[:, t : t + 1], in_=e_sb[t][:], axis=AXIS.X, op=ALU.max, negate=True)
            a_sb = ring.tile([P, M], F32, name="a_sb")
            nc.scalar.activation(
                out=a_sb[:], in_=e_sb[t][:].indirect(pos1_sb[:]), func=ACT.Exp, bias=neg_top[:, t : t + 1]
            )
            c_sb = ring.tile([P, M], F32, name="c_sb")
            nc.vector.tensor_copy(out=c_sb[:], in_=e_sb[t][:].indirect(pos2_sb[:]))
            d_sb = ring.tile([P, M], F32, name="d_sb")
            if t < 2:
                ga_sb = ring.tile([P, M], F32, name="ga_sb")
                nc.scalar.activation(out=ga_sb[:], in_=a_sb[:], func=ACT.Copy, scale=gain_sb[:, t : t + 1])
                nc.gpsimd.tensor_tensor(out=d_sb[:], in0=ga_sb[:], in1=c_sb[:], op=ALU.subtract)
                nc.gpsimd.tensor_tensor(out=y_sb[:, t, :], in0=d_sb[:], in1=c_sb[:], op=ALU.mult)
            else:
                parts = y_halves if t + 1 == PACK else [slice(0, M)]
                for cols in parts:
                    nc.vector.scalar_tensor_tensor(
                        out=d_sb[:, cols], in0=a_sb[:, cols], scalar=gain_sb[:, t : t + 1], in1=c_sb[:, cols],
                        op0=ALU.mult, op1=ALU.subtract,
                    )
                for cols in parts:
                    nc.vector.tensor_tensor(out=y_sb[:, t, cols], in0=d_sb[:, cols], in1=c_sb[:, cols], op=ALU.mult)
            nc.sync.dma_start(out=y_rows[:, t, :], in_=y_sb[:, t, :])

        y_w = held("y_w", [P, M], U32)
        y_s = held("y_s", [P, M], U8)
        y_rounded = [held("y_rounded%d" % i, [P, M // 2 * PACK], BF16) for i in range(2)]
        for rounded, cols, copy in zip(y_rounded, y_halves, (nc.scalar.copy, nc.vector.tensor_copy)):
            copy(
                out=rounded[:].rearrange("p (c i t) -> p c t i", i=4, t=PACK),
                in_=y_sb[:, :, cols].rearrange("p t (c i) -> p c t i", i=4),
            )
        words_out = out_1[0].rearrange("p m t -> p (m t)").bitcast(I32)
        for rounded, cols in reversed(list(zip(y_rounded, y_halves))):
            nc.vector.quantize_mx(out=y_w[:, cols].bitcast(FP8X4), scales=y_s[:, cols], in_=rounded[:])
            nc.sync.dma_start(out=words_out[:, cols], in_=y_w[:, cols].bitcast(I32))
        for q in range(4):
            queue = nc.scalar if q % 2 == 0 else nc.sync
            queue.dma_start(out=out_2[0, 4 * q : 4 * q + 4, :].bitcast(I32), in_=y_s[32 * q : 32 * q + 4, :].bitcast(I32))
